import numpy as np
import ml_dtypes


def mxq(x, axis, fmt="e4m3"):
    dtype, down = {"e4m3": (ml_dtypes.float8_e4m3fn, 7), "e5m2": (ml_dtypes.float8_e5m2, 14)}[fmt]
    v = np.moveaxis(np.asarray(x, np.float32).astype(ml_dtypes.bfloat16).astype(np.float64), axis, -1)
    blocks = v.reshape(v.shape[:-1] + (-1, 32))
    amax = np.abs(blocks).max(-1, keepdims=True)
    byte = np.maximum(np.where(amax > 0, np.frexp(amax)[1] - 1 + 127, 0) - down, 1)
    scale = np.exp2(byte - 127.0)
    codes = (blocks / scale).astype(np.float32).astype(dtype).astype(np.float64)
    return np.moveaxis((codes * scale).reshape(v.shape), -1, axis)


WIDE = False


def mx_kscale(k):
    if not WIDE:
        return np.ones(k)
    levels = np.array([30, -30])
    if k % 512:
        return np.exp2(np.random.permutation(np.resize(levels, k // 32))).repeat(32)
    a = np.empty((k // 512, 16))
    for p in range(k // 512):
        a[p, :8] = np.random.permutation(np.resize(levels, 8))
        for g in range(8):
            far = levels[np.abs(levels - a[p, g]) >= 10]
            a[p, g + 8] = far[np.random.randint(len(far))]
    return np.exp2(a.ravel()).repeat(32)


def f64(x):
    return np.asarray(x).astype(np.float64)


def striped(idx):
    return np.tile(np.asarray(idx).reshape(-1, 16).T, (8, 1)).astype(np.uint16)


def unstriped(offs):
    return offs[:16].T.reshape(-1).astype(np.int64)


E2M1 = np.array([0.0, 0.5, 1.0, 1.5, 2.0, 3.0, 4.0, 6.0, -0.0, -0.5, -1.0, -1.5, -2.0, -3.0, -4.0, -6.0])


def pack_weight(w, fmt):
    k, n = w.shape
    w = f64(np.asarray(w, np.float32).astype(ml_dtypes.bfloat16)).reshape(k // 32, 32, n)
    amax = np.abs(w).max(1)
    if fmt in ("e4m3", "e5m2"):
        byte = np.frexp(amax)[1] - 1 + 127 - (7 if fmt == "e4m3" else 14)
    else:
        mant, ex = np.frexp(amax / 6.0)
        byte = np.where(mant > 0.5, ex, ex - 1) + 127
    byte = np.clip(np.where(amax > 0, byte, 1), 1, 254)
    scaled = (w * np.exp2(127.0 - byte)[:, None, :]).reshape(k, n).astype(np.float32)
    by_word = np.ascontiguousarray(scaled.reshape(k // 512, 128, 4, n).transpose(0, 1, 3, 2))
    if fmt in ("e4m3", "e5m2"):
        words = by_word.astype(ml_dtypes.float8_e4m3fn if fmt == "e4m3" else ml_dtypes.float8_e5m2).view(np.uint8)
    else:
        c = by_word.astype(ml_dtypes.float4_e2m1fn).view(np.uint8) & 0xF
        words = (c[..., 0::2] | (c[..., 1::2] << 4)).reshape(k // 512, 128, 2 * n)
    return np.ascontiguousarray(words), np.ascontiguousarray(byte.astype(np.uint8).reshape(k // 512, 16, n))


def unpack_weight(words, scales, fmt):
    g, _, n = scales.shape
    words = np.ascontiguousarray(words).reshape(g, 128, n, -1)
    if fmt in ("e4m3", "e5m2"):
        vals = words.view(ml_dtypes.float8_e4m3fn if fmt == "e4m3" else ml_dtypes.float8_e5m2).astype(np.float64)
    else:
        nib = np.empty((g, 128, n, 4), np.uint8)
        nib[..., 0::2] = words & 0xF
        nib[..., 1::2] = words >> 4
        vals = E2M1[nib]
    vals = vals * np.repeat(np.exp2(scales.astype(np.float64) - 127.0), 8, axis=1)[..., None]
    return vals.transpose(0, 1, 3, 2).reshape(g * 512, n)


K, T, J, R, N = 1024, 1024, 256, 512, 256


def setup_inputs():
    n = np.random.standard_normal
    idx = np.random.permutation(T)[:J]
    idx2 = np.random.permutation(T)[:J]
    fk = mx_kscale(K)
    fr = mx_kscale(R)
    wp = pack_weight(n((K, R)) * 1 / np.sqrt(K) * fk[:, None] * fr, "e5m2")
    return {
        "xf": (n((K, T))).astype(np.float32),
        "fk": (np.random.uniform(0.5, 2.0, (K, 1)) / fk[:, None]).astype(np.float32),
        "w_words": wp[0],
        "w_scales": wp[1],
        "wb": (n((R, N)) * np.random.uniform(0.3, 1.7, (1, N)) / np.sqrt(R) / fr[:, None]).astype(np.float32),
        "rs": (0.6 * n((N, J)) + np.random.uniform(-1.0, 1.0, (N, 1))).astype(np.float32),
        "offs": striped(idx),
        "offs2": striped(idx2),
    }


def reference(xf, fk, w_words, w_scales, wb, rs, offs, offs2):
    idx = unstriped(offs)
    idx2 = unstriped(offs2)
    wu = unpack_weight(w_words, w_scales, "e5m2")
    u = (f64(xf)[:, idx] - f64(xf)[:, idx2]) * f64(fk)
    uq = mxq(u, 0, "e4m3")
    a = wu.T @ uq
    ha = np.maximum(a, 0.0)
    h1 = np.pad(ha, ((0, 0), (2, 0)))[:, :J]
    hid = ha - 0.5 * h1
    wbq = mxq(f64(wb), 0, "e5m2")
    hidq = mxq(hid, 0, "e5m2")
    p = wbq.T @ hidq
    pb = p + f64(rs)
    mn = np.mean(pb, axis=1, keepdims=True)
    d = pb - mn
    y = d / np.sqrt(np.mean(np.square(d), axis=1, keepdims=True) + 0.1)
    return y

@@ -1,0 +1,209 @@
+from contextlib import ExitStack
+
+import concourse.mybir as mybir
+
+K, T, J, R, N = 1024, 1024, 256, 512, 256
+FLOPS = 2 * K * R * J + 2 * R * N * J
+
+F32 = mybir.dt.float32
+BF16 = mybir.dt.bfloat16
+I32 = mybir.dt.int32
+U32 = mybir.dt.uint32
+U16 = mybir.dt.uint16
+U8 = mybir.dt.uint8
+E4M3 = mybir.dt.float8_e4m3fn_x4
+E5M2 = mybir.dt.float8_e5m2_x4
+ALU = mybir.AluOpType
+ACT = mybir.ActivationFunctionType
+
+P = 128
+PACK = 4
+HALF = J // 2
+LAG = 2
+
+PLANES = [(z, t) for z in range(2) for t in range(PACK)]
+
+
+def tile_list_pickgaps_lagged_levelled_kernel(tc, xf, fk, w_words, w_scales, wb, rs, offs, offs2, out):
+    nc = tc.nc
+    with ExitStack() as ctx:
+        sb = ctx.enter_context(tc.tile_pool(name="sb", bufs=1))
+        ps = ctx.enter_context(tc.psum_pool(name="ps", bufs=1))
+
+        def tile(name, shape, dtype):
+            return sb.tile(shape, dtype, name=name, align_bytes=64)
+
+        list1 = sb.tile([P, J // 16], U16, name="list1")
+        list2 = sb.tile([P, J // 16], U16, name="list2")
+        fk_sb = tile("fk_sb", [P, 2, PACK], F32)
+        x_sb = [tile("x%d" % n, [P, T], F32) for n in range(8)]
+        ws_raw = tile("ws_raw", [P, 2 * R], U8)
+        ws = tile("ws", [P, 2 * R], U8)
+        w_raw = [tile("w_raw%d" % z, [P, R], U32) for z in range(2)]
+        w_sb = [tile("w_sb%d" % z, [P, R], U32) for z in range(2)]
+        wb_raw = tile("wb_raw", [P, PACK, N], F32)
+        rs_sb = tile("rs_sb", [P, 2, J], F32)
+        ha = tile("ha", [P, PACK * (LAG + J)], F32)
+
+        nc.vector.memset(ws_raw[:].bitcast(U32), 0)
+        nc.vector.memset(ha[:, 0 : PACK * LAG], 0.0)
+
+        planes_hbm = xf.rearrange("(z p t) c -> z t p c", z=2, t=PACK)
+
+        def load_plane(n):
+            z, t = PLANES[n]
+            nc.sync.dma_start(x_sb[n][:], planes_hbm[z, t])
+
+        nc.sync.dma_start(list2[:], offs2)
+        load_plane(0)
+        nc.sync.dma_start(list1[:], offs)
+        nc.sync.dma_start(fk_sb[:], fk.rearrange("(z p t) o -> p z (t o)", z=2, t=PACK))
+        for n in range(1, 5):
+            load_plane(n)
+        scale_rows = w_scales.rearrange("z q c -> q z c").bitcast(I32)
+        for quad in range(4):
+            nc.sync.dma_start(
+                ws_raw[32 * quad : 32 * quad + 4, :].bitcast(I32).rearrange("p (z c) -> p z c", z=2),
+                scale_rows[4 * quad : 4 * quad + 4],
+            )
+        for n in range(5, 8):
+            load_plane(n)
+        for z in range(2):
+            nc.sync.dma_start(w_raw[z][:].bitcast(I32), w_words[z].rearrange("p c b -> p (c b)").bitcast(I32))
+        wb_rows = wb.rearrange("(g t i) n -> t g i n", t=PACK, i=8)
+        for t in range(PACK):
+            nc.sync.dma_start(wb_raw[:, t, :], wb_rows[t])
+        nc.sync.dma_start(rs_sb[:], rs.rearrange("(m p) j -> p m j", p=P))
+
+        second = [tile("second%d" % n, [P, J], F32) for n in range(8)]
+        first = [tile("first%d" % n, [P, HALF], F32) for n in range(7)]
+        gap = [tile("gap%d" % n, [P, J], F32) for n in range(8)]
+        u1_bf = [tile("u1_bf%d" % h, [P, HALF, PACK], BF16) for h in range(2)]
+        u1_codes = [tile("u1_codes%d" % h, [P, HALF], U32) for h in range(2)]
+        u1_scales = [tile("u1_scales%d" % h, [P, HALF], U8) for h in range(2)]
+        u0_bf = tile("u0_bf", [P, J, PACK], BF16)
+        u0_codes = tile("u0_codes", [P, J], U32)
+        u0_scales = tile("u0_scales", [P, J], U8)
+
+        def pick(dst, n, entries, lo, hi):
+            nc.scalar.activation(dst[:, lo:hi], x_sb[n][:].indirect(entries[:, lo // 16 : hi // 16]), ACT.Copy)
+
+        def pick_gap(n, lo, hi):
+            nc.vector.tensor_tensor(
+                gap[n][:, lo:hi], x_sb[n][:].indirect(list1[:, lo // 16 : hi // 16]), second[n][:, lo:hi], ALU.subtract
+            )
+
+        def scale(n, h):
+            z, t = PLANES[n]
+            cols = slice(h * HALF, (h + 1) * HALF)
+            dst = u0_bf[:, cols, t] if z == 0 else u1_bf[h][:, :, t]
+            nc.vector.tensor_scalar(dst, gap[n][:, cols], fk_sb[:, z, t : t + 1], None, ALU.mult)
+
+        def quantise(codes, scales, values, fmt):
+            nc.vector.quantize_mx(codes.bitcast(fmt), scales, values)
+
+        for n in range(7):
+            pick(second[n], n, list2, 0, J)
+            pick(first[n], n, list1, 0, HALF)
+            pick_gap(n, HALF, J)
+            nc.vector.tensor_tensor(gap[n][:, 0:HALF], first[n][:], second[n][:, 0:HALF], ALU.subtract)
+            scale(n, 1)
+            scale(n, 0)
+            if n == 4:
+                quantise(u0_codes[:], u0_scales[:], u0_bf[:].rearrange("p j t -> p (j t)"), E4M3)
+                nc.vector.tensor_copy(
+                    ws[:].bitcast(I32).rearrange("p (z t g e) -> p z t g e", z=2, t=PACK, e=2),
+                    ws_raw[:].bitcast(I32).rearrange("p (z g t e) -> p z t g e", z=2, t=PACK, e=2),
+                )
+        for h in range(2):
+            pick(second[7], 7, list2, h * HALF, (h + 1) * HALF)
+            pick_gap(7, h * HALF, (h + 1) * HALF)
+        for h in range(2):
+            scale(7, h)
+        for h in range(2):
+            quantise(u1_codes[h][:], u1_scales[h][:], u1_bf[h][:].rearrange("p j t -> p (j t)"), E4M3)
+        for z in range(2):
+            nc.scalar.copy(
+                w_sb[z][:].rearrange("p (t g i) -> p g t i", t=PACK, i=8),
+                w_raw[z][:].rearrange("p (g t i) -> p g t i", t=PACK, i=8),
+            )
+
+        a_ps = [ps.tile([P, PACK, HALF], F32, name="a_ps%d" % h) for h in range(2)]
+        for h in range(2):
+            cols = slice(h * HALF, (h + 1) * HALF)
+            for z in range(2):
+                codes = u0_codes[:, cols] if z == 0 else u1_codes[h][:]
+                scales = u0_scales[:, cols] if z == 0 else u1_scales[h][:]
+                for t in range(PACK):
+                    nc.tensor.matmul_mx(
+                        a_ps[h][:, t, :],
+                        lhsT=w_sb[z][:, t * P : (t + 1) * P].bitcast(E5M2),
+                        lhsT_scale=ws[:, z * R + t * P : z * R + (t + 1) * P],
+                        rhs=codes.bitcast(E4M3),
+                        rhs_scale=scales,
+                        start=(z == 0 and t == 0),
+                        stop=(z == 1 and t == PACK - 1),
+                    )
+
+        wb_bf = tile("wb_bf", [P, N, PACK], BF16)
+        wb_codes = tile("wb_codes", [P, N], U32)
+        wb_scales = tile("wb_scales", [P, N], U8)
+        nc.vector.tensor_copy(
+            wb_bf[:].rearrange("p (c i) t -> p c t i", i=4), wb_raw[:].rearrange("p t (c i) -> p c t i", i=4)
+        )
+        quantise(wb_codes[:], wb_scales[:], wb_bf[:].rearrange("p n t -> p (n t)"), E5M2)
+
+        staged = wb_bf[:].rearrange("p n t -> p (n t)")
+        hid_bf = [staged[:, h * HALF * PACK : (h + 1) * HALF * PACK] for h in range(2)]
+        hid_codes = [tile("hid_codes%d" % h, [P, HALF], U32) for h in range(2)]
+        hid_scales = [tile("hid_scales%d" % h, [P, HALF], U8) for h in range(2)]
+        p_ps = [[ps.tile([P, HALF], F32, name="p_ps%d%d" % (h, m)) for m in range(2)] for h in range(2)]
+        pb = [tile("pb%d" % m, [P, J], F32) for m in range(2)]
+        stats = [tile("stats%d" % m, [P, 2, 6], F32) for m in range(2)]
+        mean_var = tile("mean_var", [P, 2, 2], F32)
+        centred = tile("centred", [P, J], F32)
+        inv = tile("inv", [P, 2], F32)
+        y = [tile("y%d" % m, [P, J], F32) for m in range(2)]
+
+        piece = HALF // 2
+        for h in range(2):
+            for q in range(2):
+                j0 = h * HALF + q * piece
+                nc.scalar.activation(
+                    ha[:, PACK * (LAG + j0) : PACK * (LAG + j0 + piece)].rearrange("p (j t) -> p j t", t=PACK),
+                    a_ps[h][:, :, q * piece : (q + 1) * piece].rearrange("p t j -> p j t"),
+                    ACT.Relu,
+                )
+                nc.vector.scalar_tensor_tensor(
+                    hid_bf[h][:, PACK * q * piece : PACK * (q + 1) * piece],
+                    ha[:, PACK * j0 : PACK * (j0 + piece)],
+                    -0.5,
+                    ha[:, PACK * (LAG + j0) : PACK * (LAG + j0 + piece)],
+                    ALU.mult,
+                    ALU.add,
+                )
+            quantise(hid_codes[h][:], hid_scales[h][:], hid_bf[h], E5M2)
+            for m in range(2):
+                nc.tensor.matmul_mx(
+                    p_ps[h][m][:],
+                    lhsT=wb_codes[:, m * P : (m + 1) * P].bitcast(E5M2),
+                    lhsT_scale=wb_scales[:, m * P : (m + 1) * P],
+                    rhs=hid_codes[h][:].bitcast(E5M2),
+                    rhs_scale=hid_scales[h][:],
+                    start=True,
+                    stop=True,
+                )
+        for h in range(2):
+            cols = slice(h * HALF, (h + 1) * HALF)
+            for m in range(2):
+                nc.vector.tensor_tensor(pb[m][:, cols], p_ps[h][m][:], rs_sb[:, m, cols], ALU.add)
+            for m in range(2):
+                nc.vector.bn_stats(stats[m][:, h, :], pb[m][:, cols])
+        for m in range(2):
+            nc.vector.bn_aggr(mean_var[:, m, :], stats[m][:].rearrange("p h s -> p (h s)"))
+        nc.scalar.activation(inv[:], mean_var[:, :, 1], ACT.Abs_reciprocal_sqrt, bias=0.1)
+        nc.vector.tensor_scalar(centred[:], pb[1][:], mean_var[:, 1, 0:1], None, ALU.subtract)
+        nc.vector.tensor_scalar(y[0][:], pb[0][:], mean_var[:, 0, 0:1], inv[:, 0:1], ALU.subtract, ALU.mult)
+        nc.sync.dma_start(out[0:P, :], y[0][:])
+        nc.scalar.activation(y[1][:], centred[:], ACT.Copy, scale=inv[:, 1:2])
+        nc.scalar.dma_start(out[P : 2 * P, :], y[1][:])

@@ -48,6 +48,11 @@ def tile_list_pickgaps_lagged_levelled_kernel(tc, xf, fk, w_words, w_scales, wb,
         nc.vector.memset(ws_raw[:].bitcast(U32), 0)
         nc.vector.memset(ha[:, 0 : PACK * LAG], 0.0)
 
+        one = tile("one", [P, 1], F32)
+        warm = tile("warm", [P, 1], F32)
+        nc.vector.memset(one[:], 1.0)
+        nc.scalar.activation(warm[:], one[:], ACT.Abs_reciprocal_sqrt)
+
         planes_hbm = xf.rearrange("(z p t) c -> z t p c", z=2, t=PACK)
 
         def load_plane(n):

from contextlib import ExitStack

import concourse.mybir as mybir

K, T, J, R, N = 1024, 1024, 256, 512, 256
FLOPS = 2 * K * R * J + 2 * R * N * J

F32 = mybir.dt.float32
BF16 = mybir.dt.bfloat16
I32 = mybir.dt.int32
U32 = mybir.dt.uint32
U16 = mybir.dt.uint16
U8 = mybir.dt.uint8
E4M3 = mybir.dt.float8_e4m3fn_x4
E5M2 = mybir.dt.float8_e5m2_x4
ALU = mybir.AluOpType
ACT = mybir.ActivationFunctionType

P = 128
PACK = 4
HALF = J // 2
LAG = 2

PLANES = [(z, t) for z in range(2) for t in range(PACK)]


def tile_list_pickgaps_lagged_levelled_kernel(tc, xf, fk, w_words, w_scales, wb, rs, offs, offs2, out):
    nc = tc.nc
    with ExitStack() as ctx:
        sb = ctx.enter_context(tc.tile_pool(name="sb", bufs=1))
        ps = ctx.enter_context(tc.psum_pool(name="ps", bufs=1))

        def tile(name, shape, dtype):
            return sb.tile(shape, dtype, name=name, align_bytes=64)

        list1 = sb.tile([P, J // 16], U16, name="list1")
        list2 = sb.tile([P, J // 16], U16, name="list2")
        fk_sb = tile("fk_sb", [P, 2, PACK], F32)
        x_sb = [tile("x%d" % n, [P, T], F32) for n in range(8)]
        ws_raw = tile("ws_raw", [P, 2 * R], U8)
        ws = tile("ws", [P, 2 * R], U8)
        w_raw = [tile("w_raw%d" % z, [P, R], U32) for z in range(2)]
        w_sb = [tile("w_sb%d" % z, [P, R], U32) for z in range(2)]
        wb_raw = tile("wb_raw", [P, PACK, N], F32)
        rs_sb = tile("rs_sb", [P, 2, J], F32)
        ha = tile("ha", [P, PACK * (LAG + J)], F32)

        nc.vector.memset(ws_raw[:].bitcast(U32), 0)
        nc.vector.memset(ha[:, 0 : PACK * LAG], 0.0)

        one = tile("one", [P, 1], F32)
        warm = tile("warm", [P, 1], F32)
        nc.vector.memset(one[:], 1.0)
        nc.scalar.activation(warm[:], one[:], ACT.Abs_reciprocal_sqrt)

        planes_hbm = xf.rearrange("(z p t) c -> z t p c", z=2, t=PACK)

        def load_plane(n):
            z, t = PLANES[n]
            nc.sync.dma_start(x_sb[n][:], planes_hbm[z, t])

        nc.sync.dma_start(list2[:], offs2)
        load_plane(0)
        nc.sync.dma_start(list1[:], offs)
        nc.sync.dma_start(fk_sb[:], fk.rearrange("(z p t) o -> p z (t o)", z=2, t=PACK))
        for n in range(1, 5):
            load_plane(n)
        scale_rows = w_scales.rearrange("z q c -> q z c").bitcast(I32)
        for quad in range(4):
            nc.sync.dma_start(
                ws_raw[32 * quad : 32 * quad + 4, :].bitcast(I32).rearrange("p (z c) -> p z c", z=2),
                scale_rows[4 * quad : 4 * quad + 4],
            )
        for n in range(5, 8):
            load_plane(n)
        for z in range(2):
            nc.sync.dma_start(w_raw[z][:].bitcast(I32), w_words[z].rearrange("p c b -> p (c b)").bitcast(I32))
        wb_rows = wb.rearrange("(g t i) n -> t g i n", t=PACK, i=8)
        for t in range(PACK):
            nc.sync.dma_start(wb_raw[:, t, :], wb_rows[t])
        nc.sync.dma_start(rs_sb[:], rs.rearrange("(m p) j -> p m j", p=P))

        second = [tile("second%d" % n, [P, J], F32) for n in range(8)]
        first = [tile("first%d" % n, [P, HALF], F32) for n in range(7)]
        gap = [tile("gap%d" % n, [P, J], F32) for n in range(8)]
        u1_bf = [tile("u1_bf%d" % h, [P, HALF, PACK], BF16) for h in range(2)]
        u1_codes = [tile("u1_codes%d" % h, [P, HALF], U32) for h in range(2)]
        u1_scales = [tile("u1_scales%d" % h, [P, HALF], U8) for h in range(2)]
        u0_bf = tile("u0_bf", [P, J, PACK], BF16)
        u0_codes = tile("u0_codes", [P, J], U32)
        u0_scales = tile("u0_scales", [P, J], U8)

        def pick(dst, n, entries, lo, hi):
            nc.scalar.activation(dst[:, lo:hi], x_sb[n][:].indirect(entries[:, lo // 16 : hi // 16]), ACT.Copy)

        def pick_gap(n, lo, hi):
            nc.vector.tensor_tensor(
                gap[n][:, lo:hi], x_sb[n][:].indirect(list1[:, lo // 16 : hi // 16]), second[n][:, lo:hi], ALU.subtract
            )

        def scale(n, h):
            z, t = PLANES[n]
            cols = slice(h * HALF, (h + 1) * HALF)
            dst = u0_bf[:, cols, t] if z == 0 else u1_bf[h][:, :, t]
            nc.vector.tensor_scalar(dst, gap[n][:, cols], fk_sb[:, z, t : t + 1], None, ALU.mult)

        def quantise(codes, scales, values, fmt):
            nc.vector.quantize_mx(codes.bitcast(fmt), scales, values)

        for n in range(7):
            pick(second[n], n, list2, 0, J)
            pick(first[n], n, list1, 0, HALF)
            pick_gap(n, HALF, J)
            nc.vector.tensor_tensor(gap[n][:, 0:HALF], first[n][:], second[n][:, 0:HALF], ALU.subtract)
            scale(n, 1)
            scale(n, 0)
            if n == 4:
                quantise(u0_codes[:], u0_scales[:], u0_bf[:].rearrange("p j t -> p (j t)"), E4M3)
                nc.vector.tensor_copy(
                    ws[:].bitcast(I32).rearrange("p (z t g e) -> p z t g e", z=2, t=PACK, e=2),
                    ws_raw[:].bitcast(I32).rearrange("p (z g t e) -> p z t g e", z=2, t=PACK, e=2),
                )
        for h in range(2):
            pick(second[7], 7, list2, h * HALF, (h + 1) * HALF)
            pick_gap(7, h * HALF, (h + 1) * HALF)
        for h in range(2):
            scale(7, h)
        for h in range(2):
            quantise(u1_codes[h][:], u1_scales[h][:], u1_bf[h][:].rearrange("p j t -> p (j t)"), E4M3)
        for z in range(2):
            nc.scalar.copy(
                w_sb[z][:].rearrange("p (t g i) -> p g t i", t=PACK, i=8),
                w_raw[z][:].rearrange("p (g t i) -> p g t i", t=PACK, i=8),
            )

        a_ps = [ps.tile([P, PACK, HALF], F32, name="a_ps%d" % h) for h in range(2)]
        for h in range(2):
            cols = slice(h * HALF, (h + 1) * HALF)
            for z in range(2):
                codes = u0_codes[:, cols] if z == 0 else u1_codes[h][:]
                scales = u0_scales[:, cols] if z == 0 else u1_scales[h][:]
                for t in range(PACK):
                    nc.tensor.matmul_mx(
                        a_ps[h][:, t, :],
                        lhsT=w_sb[z][:, t * P : (t + 1) * P].bitcast(E5M2),
                        lhsT_scale=ws[:, z * R + t * P : z * R + (t + 1) * P],
                        rhs=codes.bitcast(E4M3),
                        rhs_scale=scales,
                        start=(z == 0 and t == 0),
                        stop=(z == 1 and t == PACK - 1),
                    )

        wb_bf = tile("wb_bf", [P, N, PACK], BF16)
        wb_codes = tile("wb_codes", [P, N], U32)
        wb_scales = tile("wb_scales", [P, N], U8)
        nc.vector.tensor_copy(
            wb_bf[:].rearrange("p (c i) t -> p c t i", i=4), wb_raw[:].rearrange("p t (c i) -> p c t i", i=4)
        )
        quantise(wb_codes[:], wb_scales[:], wb_bf[:].rearrange("p n t -> p (n t)"), E5M2)

        staged = wb_bf[:].rearrange("p n t -> p (n t)")
        hid_bf = [staged[:, h * HALF * PACK : (h + 1) * HALF * PACK] for h in range(2)]
        hid_codes = [tile("hid_codes%d" % h, [P, HALF], U32) for h in range(2)]
        hid_scales = [tile("hid_scales%d" % h, [P, HALF], U8) for h in range(2)]
        p_ps = [[ps.tile([P, HALF], F32, name="p_ps%d%d" % (h, m)) for m in range(2)] for h in range(2)]
        pb = [tile("pb%d" % m, [P, J], F32) for m in range(2)]
        stats = [tile("stats%d" % m, [P, 2, 6], F32) for m in range(2)]
        mean_var = tile("mean_var", [P, 2, 2], F32)
        centred = tile("centred", [P, J], F32)
        inv = tile("inv", [P, 2], F32)
        y = [tile("y%d" % m, [P, J], F32) for m in range(2)]

        piece = HALF // 2
        for h in range(2):
            for q in range(2):
                j0 = h * HALF + q * piece
                nc.scalar.activation(
                    ha[:, PACK * (LAG + j0) : PACK * (LAG + j0 + piece)].rearrange("p (j t) -> p j t", t=PACK),
                    a_ps[h][:, :, q * piece : (q + 1) * piece].rearrange("p t j -> p j t"),
                    ACT.Relu,
                )
                nc.vector.scalar_tensor_tensor(
                    hid_bf[h][:, PACK * q * piece : PACK * (q + 1) * piece],
                    ha[:, PACK * j0 : PACK * (j0 + piece)],
                    -0.5,
                    ha[:, PACK * (LAG + j0) : PACK * (LAG + j0 + piece)],
                    ALU.mult,
                    ALU.add,
                )
            quantise(hid_codes[h][:], hid_scales[h][:], hid_bf[h], E5M2)
            for m in range(2):
                nc.tensor.matmul_mx(
                    p_ps[h][m][:],
                    lhsT=wb_codes[:, m * P : (m + 1) * P].bitcast(E5M2),
                    lhsT_scale=wb_scales[:, m * P : (m + 1) * P],
                    rhs=hid_codes[h][:].bitcast(E5M2),
                    rhs_scale=hid_scales[h][:],
                    start=True,
                    stop=True,
                )
        for h in range(2):
            cols = slice(h * HALF, (h + 1) * HALF)
            for m in range(2):
                nc.vector.tensor_tensor(pb[m][:, cols], p_ps[h][m][:], rs_sb[:, m, cols], ALU.add)
            for m in range(2):
                nc.vector.bn_stats(stats[m][:, h, :], pb[m][:, cols])
        for m in range(2):
            nc.vector.bn_aggr(mean_var[:, m, :], stats[m][:].rearrange("p h s -> p (h s)"))
        nc.scalar.activation(inv[:], mean_var[:, :, 1], ACT.Abs_reciprocal_sqrt, bias=0.1)
        nc.vector.tensor_scalar(centred[:], pb[1][:], mean_var[:, 1, 0:1], None, ALU.subtract)
        nc.vector.tensor_scalar(y[0][:], pb[0][:], mean_var[:, 0, 0:1], inv[:, 0:1], ALU.subtract, ALU.mult)
        nc.sync.dma_start(out[0:P, :], y[0][:])
        nc.scalar.activation(y[1][:], centred[:], ACT.Copy, scale=inv[:, 1:2])
        nc.scalar.dma_start(out[P : 2 * P, :], y[1][:])
